import numpy as np, ml_dtypes
CORES = [3,5,19,21,35,37,51,53,67,69]
N = 10
import mx_ref
NC, G, D = 256, 2, 4
C = np.float32(0.047)
BF = ml_dtypes.bfloat16
def cut(t, i, w=512):
    return t[:, w * i:w * i + w]
def tile(rs):
    return np.stack(rs, axis=2).reshape(128, -1).astype(BF)
def act(Z):
    return [np.maximum(s * z, 0) * C for z in Z for s in (1, -1)]
def taps(w, i, e):
    return mx_ref.matmul(mx_ref.quantize(cut(w, 2 * i)), mx_ref.quantize(e[:, :4 * NC])) + mx_ref.matmul(mx_ref.quantize(cut(w, 2 * i + 1)), mx_ref.quantize(e[:, 4 * D:4 * D + 4 * NC]))
def setup_inputs(rng):
    def f(*shape):
        return mx_ref.flush((rng.standard_normal(shape, dtype=np.float32) * np.exp2(rng.integers(-2, 3, shape[:-1] + (1,)))).astype(BF))
    return {"x": f(N, 128, 4 * NC), "wa": np.broadcast_to(f(1, 128, 2 * G * 512), (N, 128, 2 * G * 512)).copy(), "wb": f(N, 128, 2 * 512)}
def setup_inputs_blocks(rng):
    d = setup_inputs(rng)
    for k in ("x", "wb"): d[k] = mx_ref.spread(d[k], rng, 2)
    return d
def setup_inputs_wide(rng):
    d = setup_inputs(rng)
    for k in ("wb",): d[k] = mx_ref.flush((d[k].astype(np.float32) * np.exp2(rng.integers(-6, 7, (N, 1, 1))).astype(np.float32)).astype(BF))
    return d
def setup_inputs_zeros(rng):
    d = setup_inputs(rng); v = d["x"].reshape(N, 128, -1, 4).copy()
    v[np.broadcast_to((rng.random((N, 1, v.shape[2], 1)) < 0.33), v.shape)] = 0
    d["x"] = v.reshape(d["x"].shape)
    return d
def reference(x, wa, wb):
    edge = lambda t, r: np.concatenate([t[(r - 1) % N][:, 4 * (NC - D):], t[r]], axis=1)
    u = [tile(act([taps(wa[r], i, edge(x, r)) for i in range(G)])) for r in range(N)]
    y = np.zeros((N, 128, NC), np.float32)
    for r in range(N):
        y[r] = taps(wb[r], 0, edge(u, r))
    return {"y": y}

@@ -1,0 +1,143 @@
+from concourse.mybir import dt, AluOpType, ActivationFunctionType
+
+C = 0.047
+NC, D = 256, 4
+H = 2 * D
+OWN = 2 * H
+NB = NC - D
+NYB = NC - H
+MIN = 128
+EU = 3 * D
+EN = MIN + D
+
+SCRATCH = {
+    "xs": ("sbuf", [128, 4 * NC], "bfloat16"),
+    "was": ("sbuf", [128, 2048], "bfloat16"),
+    "wbs": ("sbuf", [128, 1024], "bfloat16"),
+    "ub": ("sbuf", [128, 4 * NB], "bfloat16"),
+    "ue": ("sbuf", [128, 4 * EN], "bfloat16"),
+    "xe": ("sbuf", [128, OWN + NC], "float8_e4m3fn_x4"),
+    "xe_s": ("sbuf", [128, OWN + NC], "uint8"),
+    "qa": ("sbuf", [128, 512], "float8_e4m3fn_x4"),
+    "qa_s": ("sbuf", [128, 512], "uint8"),
+    "qb": ("sbuf", [128, 256], "float8_e4m3fn_x4"),
+    "qb_s": ("sbuf", [128, 256], "uint8"),
+    "qu": ("sbuf", [128, NB], "float8_e4m3fn_x4"),
+    "qu_s": ("sbuf", [128, NB], "uint8"),
+    "que": ("sbuf", [128, EN], "float8_e4m3fn_x4"),
+    "que_s": ("sbuf", [128, EN], "uint8"),
+    "yb": ("sbuf", [128, NYB], "float32"),
+    "ye": ("sbuf", [128, H], "float32"),
+    "z0": ("psum", [128, 512], "float32"),
+    "z1": ("psum", [128, 512], "float32"),
+    "z0e": ("psum", [128, 512], "float32"),
+    "z1e": ("psum", [128, 512], "float32"),
+    "pyb": ("psum", [128, 512], "float32"),
+    "pye": ("psum", [128, 512], "float32"),
+}
+SEMAPHORES = ["ld_t", "ld_x", "ld_a0", "ld_a1", "ld_b", "fill_u",
+              "q_t", "q_x", "q_a0", "q_a1", "q_b", "q_u", "q_e",
+              "s_z0", "s_z1", "s_z0e", "s_z1e", "r01", "r23", "r_edge", "s_py", "s_pye", "cy", "cye",
+              "arr", "sent", "st_b", "st_e"]
+ENGINES = 4
+
+
+def _engines(topo, src, dst):
+    bits = [b for b in range(16) if topo.mask(src, dst) >> b & 1]
+    bits = bits[::len(bits) // ENGINES]
+    return sum(1 << b for b in bits), len(bits)
+
+
+def rank_program(g, core, T, topo):
+    rank = T.rank_of(core)
+    if rank is None:
+        return
+    Alu, Act, u8 = AluOpType, ActivationFunctionType, dt.uint8
+    n = len(T.cores)
+    nxt, prv = T.cores[(rank + 1) % n], T.cores[(rank - 1) % n]
+    S = T.sem
+
+    half = 4 * (NC - MIN)
+    g.sync.dma_start(T.xs[:, half:4 * NC], T.x[:, half:4 * NC]).then_inc(S.ld_t, 16)
+    g.sync.dma_start(T.xs[:, 0:half], T.x[:, 0:half]).then_inc(S.ld_x, 16)
+    g.sync.dma_start(T.was[:, 1024:2048], T.wa[:, 1024:2048]).then_inc(S.ld_a1, 16)
+    g.scalar.wait_ge(S.fill_u, 1)
+    g.scalar.dma_start(T.was[:, 0:1024], T.wa[:, 0:1024]).then_inc(S.ld_a0, 16)
+    g.scalar.dma_start(T.wbs[:], T.wb[:]).then_inc(S.ld_b, 16)
+
+    g.vector.memset(T.ue[:, 4 * EU:4 * EN], 0.0).then_inc(S.fill_u, 1)
+    mid = OWN + NC - MIN
+    g.vector.wait_ge(S.ld_t, 16)
+    g.vector.quantize_mx(T.xe[:, mid:OWN + NC], T.xe_s[:, mid:OWN + NC], T.xs[:, half:4 * NC]).then_inc(S.q_t, 1)
+    g.vector.wait_ge(S.ld_x, 16)
+    g.vector.quantize_mx(T.xe[:, OWN:mid], T.xe_s[:, OWN:mid], T.xs[:, 0:half]).then_inc(S.q_x, 1)
+    g.vector.wait_ge(S.ld_a0, 16)
+    g.vector.quantize_mx(T.qa[:, 0:256], T.qa_s[:, 0:256], T.was[:, 0:1024]).then_inc(S.q_a0, 1)
+    g.vector.wait_ge(S.ld_a1, 16)
+    g.vector.quantize_mx(T.qa[:, 256:512], T.qa_s[:, 256:512], T.was[:, 1024:2048]).then_inc(S.q_a1, 1)
+
+    rid, pid, _ = topo.addr(nxt)
+    mask, cnt = _engines(topo, core, nxt)
+    _, cnt_in = _engines(topo, prv, core)
+    end = OWN + NC
+    g.wait_ge(S.q_t, 1)
+    g.remote_dma(T.xe[:, H:OWN].bitcast(u8), T.xe[:, end - H:end].bitcast(u8), S.arr, S.sent, pid, rid, mask)
+    g.remote_dma(T.xe_s[:, H:OWN], T.xe_s[:, end - H:end], S.arr, S.sent, pid, rid, mask)
+    g.wait_ge(S.sent, 2 * cnt)
+
+    def taps(out, n_out, w, w_s, k, m, m_s, col, sem):
+        for t in (0, 1):
+            a, c = 128 * (k + t), col + D * t
+            i = g.tensor.matmul_mx(out[:, 0:n_out], w[:, a:a + 128], w_s[:, a:a + 128],
+                                   m[:, c:c + n_out], m_s[:, c:c + n_out], t == 0, t == 1)
+        i.then_inc(sem, 1)
+
+    def vec_pair(dst, b, lim, z, sem):
+        g.vector.tensor_scalar(dst[:, b:4 * lim:4], z[:, 0:lim], 0.0, C, Alu.max, Alu.mult).then_inc(sem, 1)
+        g.vector.tensor_scalar(dst[:, b + 1:4 * lim:4], z[:, 0:lim], -C, 0.0, Alu.mult, Alu.max).then_inc(sem, 1)
+
+    g.tensor.wait_ge(S.q_t, 1)
+    g.tensor.wait_ge(S.q_x, 1)
+    g.tensor.wait_ge(S.q_a0, 1)
+    taps(T.z0, NB, T.qa, T.qa_s, 0, T.xe, T.xe_s, OWN, S.s_z0)
+    g.tensor.wait_ge(S.q_a1, 1)
+    taps(T.z1, NB, T.qa, T.qa_s, 2, T.xe, T.xe_s, OWN, S.s_z1)
+
+    g.vector.wait_ge(S.s_z0, 1)
+    vec_pair(T.ub, 0, NB, T.z0, S.r01)
+    g.scalar.wait_ge(S.s_z1, 1)
+    g.scalar.activation(T.ub[:, 2:4 * NB:4], T.z1[:, 0:NB], Act.Relu, scale=C).then_inc(S.r23, 1)
+    g.scalar.activation(T.ub[:, 3:4 * NB:4], T.z1[:, 0:NB], Act.Relu, scale=-C).then_inc(S.r23, 1)
+    g.vector.wait_ge(S.ld_b, 16)
+    g.vector.quantize_mx(T.qb[:], T.qb_s[:], T.wbs[:]).then_inc(S.q_b, 1)
+    g.vector.wait_ge(S.r01, 2)
+    g.vector.wait_ge(S.r23, 2)
+    g.vector.quantize_mx(T.qu[:], T.qu_s[:], T.ub[:]).then_inc(S.q_u, 1)
+
+    g.tensor.wait_ge(S.q_b, 1)
+    g.tensor.wait_ge(S.q_u, 1)
+    taps(T.pyb, NYB, T.qb, T.qb_s, 0, T.qu, T.qu_s, 0, S.s_py)
+
+    g.scalar.wait_ge(S.s_py, 1)
+    g.scalar.activation(T.yb[:], T.pyb[:, 0:NYB], Act.Copy).then_inc(S.cy, 1)
+    g.scalar.wait_ge(S.cy, 1)
+    g.scalar.dma_start(T.y[:, H:NC], T.yb[:]).then_inc(S.st_b, 16)
+    g.scalar.wait_ge(S.st_b, 16)
+
+    g.tensor.wait_ge(S.arr, 2 * cnt_in)
+    taps(T.z0e, MIN, T.qa, T.qa_s, 0, T.xe, T.xe_s, H, S.s_z0e)
+    taps(T.z1e, MIN, T.qa, T.qa_s, 2, T.xe, T.xe_s, H, S.s_z1e)
+    g.vector.wait_ge(S.s_z0e, 1)
+    vec_pair(T.ue, 0, EU, T.z0e, S.r_edge)
+    g.vector.wait_ge(S.s_z1e, 1)
+    vec_pair(T.ue, 2, EU, T.z1e, S.r_edge)
+    g.vector.wait_ge(S.fill_u, 1)
+    g.vector.wait_ge(S.r_edge, 4)
+    g.vector.quantize_mx(T.que[:], T.que_s[:], T.ue[:]).then_inc(S.q_e, 1)
+    g.tensor.wait_ge(S.q_e, 1)
+    taps(T.pye, MIN, T.qb, T.qb_s, 0, T.que, T.que_s, 0, S.s_pye)
+    g.vector.wait_ge(S.s_pye, 1)
+    g.vector.tensor_copy(T.ye[:], T.pye[:, 0:H]).then_inc(S.cye, 1)
+    g.sync.wait_ge(S.cye, 1)
+    g.sync.dma_start(T.y[:, 0:H], T.ye[:]).then_inc(S.st_e, 16)
+    g.sync.wait_ge(S.st_e, 16)

@@ -4,42 +4,41 @@ C = 0.047
 NC, D = 256, 4
 H = 2 * D
 OWN = 2 * H
-NB = NC - D
-NYB = NC - H
 MIN = 128
-EU = 3 * D
-EN = MIN + D
+CUT = 60
+PARTS = ((CUT, NC), (0, CUT))
+HI, LO = 0, 1
+ENGINES = 8
+
+
+def _part(a, b):
+    w = b - a + D
+    ny = max(MIN, b - a)
+    return w, max(MIN, w), ny, ny + D
+
 
 SCRATCH = {
     "xs": ("sbuf", [128, 4 * NC], "bfloat16"),
     "was": ("sbuf", [128, 2048], "bfloat16"),
     "wbs": ("sbuf", [128, 1024], "bfloat16"),
-    "ub": ("sbuf", [128, 4 * NB], "bfloat16"),
-    "ue": ("sbuf", [128, 4 * EN], "bfloat16"),
     "xe": ("sbuf", [128, OWN + NC], "float8_e4m3fn_x4"),
     "xe_s": ("sbuf", [128, OWN + NC], "uint8"),
     "qa": ("sbuf", [128, 512], "float8_e4m3fn_x4"),
     "qa_s": ("sbuf", [128, 512], "uint8"),
     "qb": ("sbuf", [128, 256], "float8_e4m3fn_x4"),
     "qb_s": ("sbuf", [128, 256], "uint8"),
-    "qu": ("sbuf", [128, NB], "float8_e4m3fn_x4"),
-    "qu_s": ("sbuf", [128, NB], "uint8"),
-    "que": ("sbuf", [128, EN], "float8_e4m3fn_x4"),
-    "que_s": ("sbuf", [128, EN], "uint8"),
-    "yb": ("sbuf", [128, NYB], "float32"),
-    "ye": ("sbuf", [128, H], "float32"),
-    "z0": ("psum", [128, 512], "float32"),
-    "z1": ("psum", [128, 512], "float32"),
-    "z0e": ("psum", [128, 512], "float32"),
-    "z1e": ("psum", [128, 512], "float32"),
-    "pyb": ("psum", [128, 512], "float32"),
-    "pye": ("psum", [128, 512], "float32"),
 }
 SEMAPHORES = ["ld_t", "ld_x", "ld_a0", "ld_a1", "ld_b", "fill_u",
-              "q_t", "q_x", "q_a0", "q_a1", "q_b", "q_u", "q_e",
-              "s_z0", "s_z1", "s_z0e", "s_z1e", "r01", "r23", "r_edge", "s_py", "s_pye", "cy", "cye",
-              "arr", "sent", "st_b", "st_e"]
-ENGINES = 4
+              "q_t", "q_x", "q_a0", "q_a2", "q_a3", "q_b", "arr", "sent"]
+for _p, (_a, _b) in enumerate(PARTS):
+    _w, _nz, _ny, _nu = _part(_a, _b)
+    SCRATCH["u%d" % _p] = ("sbuf", [128, 4 * _nu], "bfloat16")
+    SCRATCH["qu%d" % _p] = ("sbuf", [128, _nu], "float8_e4m3fn_x4")
+    SCRATCH["qu%d_s" % _p] = ("sbuf", [128, _nu], "uint8")
+    SCRATCH["ys%d" % _p] = ("sbuf", [128, _b - _a], "float32")
+    for _z in ("z0%d", "z1%d", "py%d"):
+        SCRATCH[_z % _p] = ("psum", [128, 512], "float32")
+    SEMAPHORES += [_s % _p for _s in ("s_z0%d", "s_z1%d", "r0%d", "r1%d", "q_u%d", "s_py%d", "cy%d", "st%d")]
 
 
 def _engines(topo, src, dst):
@@ -55,89 +54,109 @@ def rank_program(g, core, T, topo):
     Alu, Act, u8 = AluOpType, ActivationFunctionType, dt.uint8
     n = len(T.cores)
     nxt, prv = T.cores[(rank + 1) % n], T.cores[(rank - 1) % n]
-    S = T.sem
+    S, v = T.sem, g.vector
 
     half = 4 * (NC - MIN)
     g.sync.dma_start(T.xs[:, half:4 * NC], T.x[:, half:4 * NC]).then_inc(S.ld_t, 16)
     g.sync.dma_start(T.xs[:, 0:half], T.x[:, 0:half]).then_inc(S.ld_x, 16)
     g.sync.dma_start(T.was[:, 1024:2048], T.wa[:, 1024:2048]).then_inc(S.ld_a1, 16)
+    g.sync.dma_start(T.wbs[:], T.wb[:]).then_inc(S.ld_b, 16)
     g.scalar.wait_ge(S.fill_u, 1)
     g.scalar.dma_start(T.was[:, 0:1024], T.wa[:, 0:1024]).then_inc(S.ld_a0, 16)
-    g.scalar.dma_start(T.wbs[:], T.wb[:]).then_inc(S.ld_b, 16)
 
-    g.vector.memset(T.ue[:, 4 * EU:4 * EN], 0.0).then_inc(S.fill_u, 1)
+    w, _, _, nu = _part(*PARTS[LO])
+    v.memset(T["u%d" % LO][:, 4 * w:4 * nu], 0.0).then_inc(S.fill_u, 1)
     mid = OWN + NC - MIN
-    g.vector.wait_ge(S.ld_t, 16)
-    g.vector.quantize_mx(T.xe[:, mid:OWN + NC], T.xe_s[:, mid:OWN + NC], T.xs[:, half:4 * NC]).then_inc(S.q_t, 1)
-    g.vector.wait_ge(S.ld_x, 16)
-    g.vector.quantize_mx(T.xe[:, OWN:mid], T.xe_s[:, OWN:mid], T.xs[:, 0:half]).then_inc(S.q_x, 1)
-    g.vector.wait_ge(S.ld_a0, 16)
-    g.vector.quantize_mx(T.qa[:, 0:256], T.qa_s[:, 0:256], T.was[:, 0:1024]).then_inc(S.q_a0, 1)
-    g.vector.wait_ge(S.ld_a1, 16)
-    g.vector.quantize_mx(T.qa[:, 256:512], T.qa_s[:, 256:512], T.was[:, 1024:2048]).then_inc(S.q_a1, 1)
+    end = OWN + NC
+    v.wait_ge(S.ld_t, 16)
+    v.quantize_mx(T.xe[:, mid:end], T.xe_s[:, mid:end], T.xs[:, half:4 * NC]).then_inc(S.q_t, 1)
+    v.wait_ge(S.ld_x, 16)
+    v.quantize_mx(T.xe[:, OWN:mid], T.xe_s[:, OWN:mid], T.xs[:, 0:half]).then_inc(S.q_x, 1)
+
+    def codes(q, q_s, src, k, m, sem):
+        v.quantize_mx(q[:, MIN * k:MIN * m], q_s[:, MIN * k:MIN * m], src[:, 4 * MIN * k:4 * MIN * m]).then_inc(sem, 1)
+    v.wait_ge(S.ld_a0, 16)
+    codes(T.qa, T.qa_s, T.was, 0, 2, S.q_a0)
+    v.wait_ge(S.ld_a1, 16)
+    codes(T.qa, T.qa_s, T.was, 2, 3, S.q_a2)
+    codes(T.qa, T.qa_s, T.was, 3, 4, S.q_a3)
 
     rid, pid, _ = topo.addr(nxt)
     mask, cnt = _engines(topo, core, nxt)
     _, cnt_in = _engines(topo, prv, core)
-    end = OWN + NC
     g.wait_ge(S.q_t, 1)
     g.remote_dma(T.xe[:, H:OWN].bitcast(u8), T.xe[:, end - H:end].bitcast(u8), S.arr, S.sent, pid, rid, mask)
     g.remote_dma(T.xe_s[:, H:OWN], T.xe_s[:, end - H:end], S.arr, S.sent, pid, rid, mask)
     g.wait_ge(S.sent, 2 * cnt)
 
-    def taps(out, n_out, w, w_s, k, m, m_s, col, sem):
+    def taps(out, m, w, w_s, k, src, src_s, col, sem, waits=(None, None)):
         for t in (0, 1):
-            a, c = 128 * (k + t), col + D * t
-            i = g.tensor.matmul_mx(out[:, 0:n_out], w[:, a:a + 128], w_s[:, a:a + 128],
-                                   m[:, c:c + n_out], m_s[:, c:c + n_out], t == 0, t == 1)
+            if waits[t]:
+                g.tensor.wait_ge(S[waits[t]], 1)
+            a, c = MIN * (k + t), col + D * t
+            i = g.tensor.matmul_mx(out[:, 0:m], w[:, a:a + MIN], w_s[:, a:a + MIN],
+                                   src[:, c:c + m], src_s[:, c:c + m], t == 0, t == 1)
         i.then_inc(sem, 1)
 
-    def vec_pair(dst, b, lim, z, sem):
-        g.vector.tensor_scalar(dst[:, b:4 * lim:4], z[:, 0:lim], 0.0, C, Alu.max, Alu.mult).then_inc(sem, 1)
-        g.vector.tensor_scalar(dst[:, b + 1:4 * lim:4], z[:, 0:lim], -C, 0.0, Alu.mult, Alu.max).then_inc(sem, 1)
+    def layer1(p, i, waits=(None, None)):
+        a, b = PARTS[p]
+        taps(T["z%d%d" % (i, p)], _part(a, b)[1], T.qa, T.qa_s, 2 * i, T.xe, T.xe_s, OWN - H + a,
+             S["s_z%d%d" % (i, p)], waits)
+
+    def layer2(p):
+        a, b = PARTS[p]
+        g.tensor.wait_ge(S["q_u%d" % p], 1)
+        taps(T["py%d" % p], _part(a, b)[2], T.qb, T.qb_s, 0, T["qu%d" % p], T["qu%d_s" % p], 0, S["s_py%d" % p])
+
+    def vec_pair(p, i):
+        w = _part(*PARTS[p])[0]
+        z, u, sem = T["z%d%d" % (i, p)], T["u%d" % p], S["r%d%d" % (i, p)]
+        v.wait_ge(S["s_z%d%d" % (i, p)], 1)
+        v.tensor_scalar(u[:, 2 * i:4 * w:4], z[:, 0:w], 0.0, C, Alu.max, Alu.mult).then_inc(sem, 1)
+        v.tensor_scalar(u[:, 2 * i + 1:4 * w:4], z[:, 0:w], -C, 0.0, Alu.mult, Alu.max).then_inc(sem, 1)
+
+    def scalar_pair(p, i):
+        w = _part(*PARTS[p])[0]
+        z, u, sem = T["z%d%d" % (i, p)], T["u%d" % p], S["r%d%d" % (i, p)]
+        g.scalar.wait_ge(S["s_z%d%d" % (i, p)], 1)
+        g.scalar.activation(u[:, 2 * i:4 * w:4], z[:, 0:w], Act.Relu, scale=C).then_inc(sem, 1)
+        g.scalar.activation(u[:, 2 * i + 1:4 * w:4], z[:, 0:w], Act.Relu, scale=-C).then_inc(sem, 1)
+
+    def quant_u(p):
+        v.wait_ge(S["r0%d" % p], 2)
+        v.wait_ge(S["r1%d" % p], 2)
+        v.quantize_mx(T["qu%d" % p][:], T["qu%d_s" % p][:], T["u%d" % p][:]).then_inc(S["q_u%d" % p], 1)
+
+    def store(p, queue):
+        a, b = PARTS[p]
+        queue.wait_ge(S["cy%d" % p], 1)
+        queue.dma_start(T.y[:, a:b], T["ys%d" % p][:]).then_inc(S["st%d" % p], 16)
+        queue.wait_ge(S["st%d" % p], 16)
 
     g.tensor.wait_ge(S.q_t, 1)
     g.tensor.wait_ge(S.q_x, 1)
-    g.tensor.wait_ge(S.q_a0, 1)
-    taps(T.z0, NB, T.qa, T.qa_s, 0, T.xe, T.xe_s, OWN, S.s_z0)
-    g.tensor.wait_ge(S.q_a1, 1)
-    taps(T.z1, NB, T.qa, T.qa_s, 2, T.xe, T.xe_s, OWN, S.s_z1)
-
-    g.vector.wait_ge(S.s_z0, 1)
-    vec_pair(T.ub, 0, NB, T.z0, S.r01)
-    g.scalar.wait_ge(S.s_z1, 1)
-    g.scalar.activation(T.ub[:, 2:4 * NB:4], T.z1[:, 0:NB], Act.Relu, scale=C).then_inc(S.r23, 1)
-    g.scalar.activation(T.ub[:, 3:4 * NB:4], T.z1[:, 0:NB], Act.Relu, scale=-C).then_inc(S.r23, 1)
-    g.vector.wait_ge(S.ld_b, 16)
-    g.vector.quantize_mx(T.qb[:], T.qb_s[:], T.wbs[:]).then_inc(S.q_b, 1)
-    g.vector.wait_ge(S.r01, 2)
-    g.vector.wait_ge(S.r23, 2)
-    g.vector.quantize_mx(T.qu[:], T.qu_s[:], T.ub[:]).then_inc(S.q_u, 1)
-
-    g.tensor.wait_ge(S.q_b, 1)
-    g.tensor.wait_ge(S.q_u, 1)
-    taps(T.pyb, NYB, T.qb, T.qb_s, 0, T.qu, T.qu_s, 0, S.s_py)
-
-    g.scalar.wait_ge(S.s_py, 1)
-    g.scalar.activation(T.yb[:], T.pyb[:, 0:NYB], Act.Copy).then_inc(S.cy, 1)
-    g.scalar.wait_ge(S.cy, 1)
-    g.scalar.dma_start(T.y[:, H:NC], T.yb[:]).then_inc(S.st_b, 16)
-    g.scalar.wait_ge(S.st_b, 16)
-
+    layer1(HI, 0, ("q_a0", None))
+    layer1(HI, 1, ("q_a2", "q_a3"))
     g.tensor.wait_ge(S.arr, 2 * cnt_in)
-    taps(T.z0e, MIN, T.qa, T.qa_s, 0, T.xe, T.xe_s, H, S.s_z0e)
-    taps(T.z1e, MIN, T.qa, T.qa_s, 2, T.xe, T.xe_s, H, S.s_z1e)
-    g.vector.wait_ge(S.s_z0e, 1)
-    vec_pair(T.ue, 0, EU, T.z0e, S.r_edge)
-    g.vector.wait_ge(S.s_z1e, 1)
-    vec_pair(T.ue, 2, EU, T.z1e, S.r_edge)
-    g.vector.wait_ge(S.fill_u, 1)
-    g.vector.wait_ge(S.r_edge, 4)
-    g.vector.quantize_mx(T.que[:], T.que_s[:], T.ue[:]).then_inc(S.q_e, 1)
-    g.tensor.wait_ge(S.q_e, 1)
-    taps(T.pye, MIN, T.qb, T.qb_s, 0, T.que, T.que_s, 0, S.s_pye)
-    g.vector.wait_ge(S.s_pye, 1)
-    g.vector.tensor_copy(T.ye[:], T.pye[:, 0:H]).then_inc(S.cye, 1)
-    g.sync.wait_ge(S.cye, 1)
-    g.sync.dma_start(T.y[:, 0:H], T.ye[:]).then_inc(S.st_e, 16)
-    g.sync.wait_ge(S.st_e, 16)
+    layer1(LO, 0)
+    layer1(LO, 1)
+    g.tensor.wait_ge(S.q_b, 1)
+    layer2(HI)
+    layer2(LO)
+
+    vec_pair(HI, 0)
+    scalar_pair(HI, 1)
+    v.wait_ge(S.ld_b, 16)
+    codes(T.qb, T.qb_s, T.wbs, 0, 2, S.q_b)
+    quant_u(HI)
+    vec_pair(LO, 0)
+    vec_pair(LO, 1)
+    v.wait_ge(S.fill_u, 1)
+    quant_u(LO)
+
+    g.scalar.wait_ge(S["s_py%d" % HI], 1)
+    g.scalar.activation(T["ys%d" % HI][:], T["py%d" % HI][:, 0:NC - CUT], Act.Copy).then_inc(S["cy%d" % HI], 1)
+    store(HI, g.scalar)
+    v.wait_ge(S["s_py%d" % LO], 1)
+    v.tensor_copy(T["ys%d" % LO][:], T["py%d" % LO][:, 0:CUT]).then_inc(S["cy%d" % LO], 1)
+    store(LO, g.sync)

from concourse.mybir import dt, AluOpType, ActivationFunctionType

C = 0.047
NC, D = 256, 4
H = 2 * D
OWN = 2 * H
MIN = 128
CUT = 60
PARTS = ((CUT, NC), (0, CUT))
HI, LO = 0, 1
ENGINES = 8


def _part(a, b):
    w = b - a + D
    ny = max(MIN, b - a)
    return w, max(MIN, w), ny, ny + D


SCRATCH = {
    "xs": ("sbuf", [128, 4 * NC], "bfloat16"),
    "was": ("sbuf", [128, 2048], "bfloat16"),
    "wbs": ("sbuf", [128, 1024], "bfloat16"),
    "xe": ("sbuf", [128, OWN + NC], "float8_e4m3fn_x4"),
    "xe_s": ("sbuf", [128, OWN + NC], "uint8"),
    "qa": ("sbuf", [128, 512], "float8_e4m3fn_x4"),
    "qa_s": ("sbuf", [128, 512], "uint8"),
    "qb": ("sbuf", [128, 256], "float8_e4m3fn_x4"),
    "qb_s": ("sbuf", [128, 256], "uint8"),
}
SEMAPHORES = ["ld_t", "ld_x", "ld_a0", "ld_a1", "ld_b", "fill_u",
              "q_t", "q_x", "q_a0", "q_a2", "q_a3", "q_b", "arr", "sent"]
for _p, (_a, _b) in enumerate(PARTS):
    _w, _nz, _ny, _nu = _part(_a, _b)
    SCRATCH["u%d" % _p] = ("sbuf", [128, 4 * _nu], "bfloat16")
    SCRATCH["qu%d" % _p] = ("sbuf", [128, _nu], "float8_e4m3fn_x4")
    SCRATCH["qu%d_s" % _p] = ("sbuf", [128, _nu], "uint8")
    SCRATCH["ys%d" % _p] = ("sbuf", [128, _b - _a], "float32")
    for _z in ("z0%d", "z1%d", "py%d"):
        SCRATCH[_z % _p] = ("psum", [128, 512], "float32")
    SEMAPHORES += [_s % _p for _s in ("s_z0%d", "s_z1%d", "r0%d", "r1%d", "q_u%d", "s_py%d", "cy%d", "st%d")]


def _engines(topo, src, dst):
    bits = [b for b in range(16) if topo.mask(src, dst) >> b & 1]
    bits = bits[::len(bits) // ENGINES]
    return sum(1 << b for b in bits), len(bits)


def rank_program(g, core, T, topo):
    rank = T.rank_of(core)
    if rank is None:
        return
    Alu, Act, u8 = AluOpType, ActivationFunctionType, dt.uint8
    n = len(T.cores)
    nxt, prv = T.cores[(rank + 1) % n], T.cores[(rank - 1) % n]
    S, v = T.sem, g.vector

    half = 4 * (NC - MIN)
    g.sync.dma_start(T.xs[:, half:4 * NC], T.x[:, half:4 * NC]).then_inc(S.ld_t, 16)
    g.sync.dma_start(T.xs[:, 0:half], T.x[:, 0:half]).then_inc(S.ld_x, 16)
    g.sync.dma_start(T.was[:, 1024:2048], T.wa[:, 1024:2048]).then_inc(S.ld_a1, 16)
    g.sync.dma_start(T.wbs[:], T.wb[:]).then_inc(S.ld_b, 16)
    g.scalar.wait_ge(S.fill_u, 1)
    g.scalar.dma_start(T.was[:, 0:1024], T.wa[:, 0:1024]).then_inc(S.ld_a0, 16)

    w, _, _, nu = _part(*PARTS[LO])
    v.memset(T["u%d" % LO][:, 4 * w:4 * nu], 0.0).then_inc(S.fill_u, 1)
    mid = OWN + NC - MIN
    end = OWN + NC
    v.wait_ge(S.ld_t, 16)
    v.quantize_mx(T.xe[:, mid:end], T.xe_s[:, mid:end], T.xs[:, half:4 * NC]).then_inc(S.q_t, 1)
    v.wait_ge(S.ld_x, 16)
    v.quantize_mx(T.xe[:, OWN:mid], T.xe_s[:, OWN:mid], T.xs[:, 0:half]).then_inc(S.q_x, 1)

    def codes(q, q_s, src, k, m, sem):
        v.quantize_mx(q[:, MIN * k:MIN * m], q_s[:, MIN * k:MIN * m], src[:, 4 * MIN * k:4 * MIN * m]).then_inc(sem, 1)
    v.wait_ge(S.ld_a0, 16)
    codes(T.qa, T.qa_s, T.was, 0, 2, S.q_a0)
    v.wait_ge(S.ld_a1, 16)
    codes(T.qa, T.qa_s, T.was, 2, 3, S.q_a2)
    codes(T.qa, T.qa_s, T.was, 3, 4, S.q_a3)

    rid, pid, _ = topo.addr(nxt)
    mask, cnt = _engines(topo, core, nxt)
    _, cnt_in = _engines(topo, prv, core)
    g.wait_ge(S.q_t, 1)
    g.remote_dma(T.xe[:, H:OWN].bitcast(u8), T.xe[:, end - H:end].bitcast(u8), S.arr, S.sent, pid, rid, mask)
    g.remote_dma(T.xe_s[:, H:OWN], T.xe_s[:, end - H:end], S.arr, S.sent, pid, rid, mask)
    g.wait_ge(S.sent, 2 * cnt)

    def taps(out, m, w, w_s, k, src, src_s, col, sem, waits=(None, None)):
        for t in (0, 1):
            if waits[t]:
                g.tensor.wait_ge(S[waits[t]], 1)
            a, c = MIN * (k + t), col + D * t
            i = g.tensor.matmul_mx(out[:, 0:m], w[:, a:a + MIN], w_s[:, a:a + MIN],
                                   src[:, c:c + m], src_s[:, c:c + m], t == 0, t == 1)
        i.then_inc(sem, 1)

    def layer1(p, i, waits=(None, None)):
        a, b = PARTS[p]
        taps(T["z%d%d" % (i, p)], _part(a, b)[1], T.qa, T.qa_s, 2 * i, T.xe, T.xe_s, OWN - H + a,
             S["s_z%d%d" % (i, p)], waits)

    def layer2(p):
        a, b = PARTS[p]
        g.tensor.wait_ge(S["q_u%d" % p], 1)
        taps(T["py%d" % p], _part(a, b)[2], T.qb, T.qb_s, 0, T["qu%d" % p], T["qu%d_s" % p], 0, S["s_py%d" % p])

    def vec_pair(p, i):
        w = _part(*PARTS[p])[0]
        z, u, sem = T["z%d%d" % (i, p)], T["u%d" % p], S["r%d%d" % (i, p)]
        v.wait_ge(S["s_z%d%d" % (i, p)], 1)
        v.tensor_scalar(u[:, 2 * i:4 * w:4], z[:, 0:w], 0.0, C, Alu.max, Alu.mult).then_inc(sem, 1)
        v.tensor_scalar(u[:, 2 * i + 1:4 * w:4], z[:, 0:w], -C, 0.0, Alu.mult, Alu.max).then_inc(sem, 1)

    def scalar_pair(p, i):
        w = _part(*PARTS[p])[0]
        z, u, sem = T["z%d%d" % (i, p)], T["u%d" % p], S["r%d%d" % (i, p)]
        g.scalar.wait_ge(S["s_z%d%d" % (i, p)], 1)
        g.scalar.activation(u[:, 2 * i:4 * w:4], z[:, 0:w], Act.Relu, scale=C).then_inc(sem, 1)
        g.scalar.activation(u[:, 2 * i + 1:4 * w:4], z[:, 0:w], Act.Relu, scale=-C).then_inc(sem, 1)

    def quant_u(p):
        v.wait_ge(S["r0%d" % p], 2)
        v.wait_ge(S["r1%d" % p], 2)
        v.quantize_mx(T["qu%d" % p][:], T["qu%d_s" % p][:], T["u%d" % p][:]).then_inc(S["q_u%d" % p], 1)

    def store(p, queue):
        a, b = PARTS[p]
        queue.wait_ge(S["cy%d" % p], 1)
        queue.dma_start(T.y[:, a:b], T["ys%d" % p][:]).then_inc(S["st%d" % p], 16)
        queue.wait_ge(S["st%d" % p], 16)

    g.tensor.wait_ge(S.q_t, 1)
    g.tensor.wait_ge(S.q_x, 1)
    layer1(HI, 0, ("q_a0", None))
    layer1(HI, 1, ("q_a2", "q_a3"))
    g.tensor.wait_ge(S.arr, 2 * cnt_in)
    layer1(LO, 0)
    layer1(LO, 1)
    g.tensor.wait_ge(S.q_b, 1)
    layer2(HI)
    layer2(LO)

    vec_pair(HI, 0)
    scalar_pair(HI, 1)
    v.wait_ge(S.ld_b, 16)
    codes(T.qb, T.qb_s, T.wbs, 0, 2, S.q_b)
    quant_u(HI)
    vec_pair(LO, 0)
    vec_pair(LO, 1)
    v.wait_ge(S.fill_u, 1)
    quant_u(LO)

    g.scalar.wait_ge(S["s_py%d" % HI], 1)
    g.scalar.activation(T["ys%d" % HI][:], T["py%d" % HI][:, 0:NC - CUT], Act.Copy).then_inc(S["cy%d" % HI], 1)
    store(HI, g.scalar)
    v.wait_ge(S["s_py%d" % LO], 1)
    v.tensor_copy(T["ys%d" % LO][:], T["py%d" % LO][:, 0:CUT]).then_inc(S["cy%d" % LO], 1)
    store(LO, g.sync)
